import numpy as np
import ml_dtypes


def mxq(x, axis, fmt="e4m3"):
    dtype, down = {"e4m3": (ml_dtypes.float8_e4m3fn, 7), "e5m2": (ml_dtypes.float8_e5m2, 14)}[fmt]
    v = np.moveaxis(np.asarray(x, np.float32).astype(ml_dtypes.bfloat16).astype(np.float64), axis, -1)
    blocks = v.reshape(v.shape[:-1] + (-1, 32))
    amax = np.abs(blocks).max(-1, keepdims=True)
    byte = np.maximum(np.where(amax > 0, np.frexp(amax)[1] - 1 + 127, 0) - down, 1)
    scale = np.exp2(byte - 127.0)
    codes = (blocks / scale).astype(np.float32).astype(dtype).astype(np.float64)
    return np.moveaxis((codes * scale).reshape(v.shape), -1, axis)


WIDE = False


def mx_kscale(k):
    if not WIDE:
        return np.ones(k)
    levels = np.array([10, -10, 5, -5, 0])
    if k % 512:
        return np.exp2(np.random.permutation(np.resize(levels, k // 32))).repeat(32)
    a = np.empty((k // 512, 16))
    for p in range(k // 512):
        a[p, :8] = np.random.permutation(np.resize(levels, 8))
        for g in range(8):
            far = levels[np.abs(levels - a[p, g]) >= 10]
            a[p, g + 8] = far[np.random.randint(len(far))]
    return np.exp2(a.ravel()).repeat(32)


def f64(x):
    return np.asarray(x).astype(np.float64)


def striped(idx):
    return np.tile(idx.reshape(-1, 16).T, (8, 1)).astype(np.uint16)


def unstriped(offs):
    return offs[:16].T.reshape(-1).astype(np.int64)


E2M1 = np.array([0.0, 0.5, 1.0, 1.5, 2.0, 3.0, 4.0, 6.0, -0.0, -0.5, -1.0, -1.5, -2.0, -3.0, -4.0, -6.0])


def pack_weight(w, fmt):
    k, n = w.shape
    w = f64(np.asarray(w, np.float32).astype(ml_dtypes.bfloat16)).reshape(k // 32, 32, n)
    amax = np.abs(w).max(1)
    if fmt == "e4m3":
        byte = np.frexp(amax)[1] - 1 + 127 - 7
    else:
        mant, ex = np.frexp(amax / 6.0)
        byte = np.where(mant > 0.5, ex, ex - 1) + 127
    byte = np.clip(np.where(amax > 0, byte, 1), 1, 254)
    scaled = (w * np.exp2(127.0 - byte)[:, None, :]).reshape(k, n).astype(np.float32)
    by_word = np.ascontiguousarray(scaled.reshape(k // 512, 128, 4, n).transpose(0, 1, 3, 2))
    if fmt == "e4m3":
        words = by_word.astype(ml_dtypes.float8_e4m3fn).view(np.uint8)
    else:
        c = by_word.astype(ml_dtypes.float4_e2m1fn).view(np.uint8) & 0xF
        words = (c[..., 0::2] | (c[..., 1::2] << 4)).reshape(k // 512, 128, 2 * n)
    return np.ascontiguousarray(words), np.ascontiguousarray(byte.astype(np.uint8).reshape(k // 512, 16, n))


def unpack_weight(words, scales, fmt):
    g, _, n = scales.shape
    words = np.ascontiguousarray(words).reshape(g, 128, n, -1)
    if fmt == "e4m3":
        vals = words.view(ml_dtypes.float8_e4m3fn).astype(np.float64)
    else:
        nib = np.empty((g, 128, n, 4), np.uint8)
        nib[..., 0::2] = words & 0xF
        nib[..., 1::2] = words >> 4
        vals = E2M1[nib]
    vals = vals * np.repeat(np.exp2(scales.astype(np.float64) - 127.0), 8, axis=1)[..., None]
    return vals.transpose(0, 1, 3, 2).reshape(g * 512, n)


def gelu(v):
    return 0.5 * v * (1.0 + np.tanh(np.sqrt(2.0 / np.pi) * (v + 0.044715 * v**3)))


K, K2, T, S, H, N = 1024, 512, 4096, 1024, 1024, 384

def setup_inputs():
    n = np.random.standard_normal
    s = mx_kscale(K)[:, None]
    s2 = mx_kscale(K2)[:, None]
    u = mx_kscale(H)[:, None]
    d = {}
    d["tab_words"], d["tab_scales"] = pack_weight(n((K, T)) * s, "e4m3")
    d["offs"] = striped(np.random.permutation(T)[:S])
    d["xs_words"], d["xs_scales"] = pack_weight(n((K2, S)) * s2, "e4m3")
    d["w1"] = (n((K, H)) / s * u.T / K ** 0.5).astype(np.float32)
    d["b1"] = (0.5 * n(H) * u[:, 0]).astype(np.float32)
    d["wg_words"], d["wg_scales"] = pack_weight(n((K2, H)) / s2 * u.T / K2 ** 0.5, "e2m1")
    d["wl"] = (n((H, N)) / u / H ** 0.5).astype(np.float32)
    d["wc_words"], d["wc_scales"] = pack_weight(1.5 * n((H, N)) / u / H ** 0.5, "e2m1")
    return d

def reference(tab_words, tab_scales, offs, xs_words, xs_scales, w1, b1, wg_words, wg_scales, wl, wc_words, wc_scales):
    v = unpack_weight(tab_words, tab_scales, "e4m3")[:, unstriped(offs)]
    xs = unpack_weight(xs_words, xs_scales, "e4m3")
    wg = unpack_weight(wg_words, wg_scales, "e2m1")
    wc = unpack_weight(wc_words, wc_scales, "e2m1")
    a = mxq(f64(w1), 0, "e4m3").T @ v
    h = np.maximum(a + f64(b1)[:, None], 0.0)
    b = wg.T @ xs
    z = h - b
    p = mxq(f64(wl), 0, "e4m3").T @ mxq(z, 0, "e4m3")
    q = wc.T @ mxq(h, 0, "e4m3")
    return p / (1.0 + np.abs(q))

@@ -1,0 +1,277 @@
+from contextlib import ExitStack
+
+import concourse.mybir as mybir
+
+K, K2, T, S, H, N = 1024, 512, 4096, 1024, 1024, 384
+FLOPS = 2 * S * (K * H + K2 * H + 2 * H * N)
+
+F32 = mybir.dt.float32
+BF16 = mybir.dt.bfloat16
+I32 = mybir.dt.int32
+U32 = mybir.dt.uint32
+U16 = mybir.dt.uint16
+U8 = mybir.dt.uint8
+FP8X4 = mybir.dt.float8_e4m3fn_x4
+FP4X4 = mybir.dt.float4_e2m1fn_x4
+ALU = mybir.AluOpType
+ACT = mybir.ActivationFunctionType
+
+P = 128
+PACK = 4
+KP = P * PACK
+QUADS = 4
+QROWS = 4
+CHUNK = 512
+BLK = 128
+PAIR = 2
+M_VEC = 84
+
+
+def tile_list_handicap_sheet_scores_kernel(
+    tc, tab_words, tab_scales, offs, xs_words, xs_scales, w1, b1, wg_words, wg_scales, wl, wc_words, wc_scales, out
+):
+    nc = tc.nc
+    with ExitStack() as ctx:
+        keep = ctx.enter_context(tc.tile_pool(name="keep", bufs=1))
+        ring = ctx.enter_context(tc.tile_pool(name="ring", bufs=2))
+        acc_pool = ctx.enter_context(tc.psum_pool(name="acc", bufs=6))
+        b_pool = ctx.enter_context(tc.psum_pool(name="bsum", bufs=2))
+
+        def kept(shape, dtype, name):
+            return keep.tile(shape, dtype, name=name, align_bytes=64)
+
+        offsets = keep.tile([P, S // 16], U16, name="offsets")
+        tab = [kept([P, T], U32, "tab%d" % a) for a in range(2)]
+        tab_sc = kept([P, T], U8, "tab_sc")
+        v = [kept([P, S], U32, "v%d" % a) for a in range(2)]
+        v_sc = kept([P, S], U8, "v_sc")
+        xs = kept([P, S], U32, "xs")
+        xs_sc = kept([P, S], U8, "xs_sc")
+        wg_raw = kept([P, 2 * H], U8, "wg_raw")
+        wg_sc_raw = kept([P, H], U8, "wg_sc_raw")
+        wg = kept([P, 2 * H], U8, "wg")
+        wg_sc = kept([P, H], U8, "wg_sc")
+        wc = kept([P, 2 * 2 * N], U8, "wc")
+        wc_sc = kept([P, 2 * N], U8, "wc_sc")
+        bias = kept([P, 2 * PACK], F32, "bias")
+        w1_raw = {(a, g): kept([P, PACK, KP], F32, "w1_raw%d%d" % (a, g)) for g in range(2) for a in range(2)}
+        w1_bf = {(a, g): kept([P, PACK * KP], BF16, "w1_bf%d%d" % (a, g)) for g in range(2) for a in range(2)}
+        w1q = {(a, g): kept([P, KP], U32, "w1q%d%d" % (a, g)) for g in range(2) for a in range(2)}
+        w1_sc = {(a, g): kept([P, KP], U8, "w1_sc%d%d" % (a, g)) for g in range(2) for a in range(2)}
+        wl_raw = [kept([P, PACK, N], F32, "wl_raw%d" % g) for g in range(2)]
+        wl_bf = [kept([P, PACK * N], BF16, "wl_bf%d" % g) for g in range(2)]
+        wlq = [kept([P, N], U32, "wlq%d" % g) for g in range(2)]
+        wl_sc = [kept([P, N], U8, "wl_sc%d" % g) for g in range(2)]
+        units = [(g, c) for g in range(2) for c in range(2)]
+        hq = {u: kept([P, CHUNK], U32, "hq%d%d" % u) for u in units}
+        h_sc = {u: kept([P, CHUNK], U8, "h_sc%d%d" % u) for u in units}
+        zq = {u: kept([P, CHUNK], U32, "zq%d%d" % u) for u in units}
+        z_sc = {u: kept([P, CHUNK], U8, "z_sc%d%d" % u) for u in units}
+        damp = {(c, n): kept([P, CHUNK], F32, "damp%d%d" % (c, n)) for c in range(2) for n in range(3)}
+
+        def rows(q, first=0):
+            return slice(32 * q + first, 32 * q + first + QROWS)
+
+        def load_words(tile, words, lo, hi):
+            nc.sync.dma_start(
+                out=tile[:, lo:hi].bitcast(I32), in_=words[:, lo:hi, :].rearrange("p n t -> p (n t)").bitcast(I32)
+            )
+
+        def load_w1(a, g):
+            nc.sync.dma_start(
+                out=w1_raw[a, g][:],
+                in_=w1[a * KP : (a + 1) * KP, g * KP : (g + 1) * KP].rearrange("(p j) c -> p j c", j=PACK),
+            )
+
+        def load_scales(tile, scales, first=0):
+            for q in range(QUADS):
+                nc.sync.dma_start(
+                    out=tile[rows(q, first), :].bitcast(I32), in_=scales[QROWS * q : QROWS * (q + 1), :].bitcast(I32)
+                )
+
+        for plane in (tab_sc, wg_sc_raw, xs_sc, wc_sc):
+            nc.vector.memset(plane[:].bitcast(I32), 0)
+        nc.sync.dma_start(offsets[:], offs)
+        nc.sync.dma_start(out=wg_raw[:].bitcast(I32), in_=wg_words[0].bitcast(I32))
+        load_words(tab[0], tab_words[0], 0, T // 2)
+        load_scales(tab_sc, tab_scales[0])
+        load_words(tab[0], tab_words[0], T // 2, T)
+        load_scales(tab_sc, tab_scales[1], QROWS)
+        load_words(tab[1], tab_words[1], 0, T // 2)
+        load_scales(wg_sc_raw, wg_scales[0])
+        load_words(tab[1], tab_words[1], T // 2, T)
+        load_w1(0, 0)
+        load_w1(1, 0)
+        nc.sync.dma_start(
+            out=bias[:].rearrange("p (g t) -> p g t", t=PACK), in_=b1.rearrange("(g p t) -> p g t", g=2, t=PACK)
+        )
+        load_words(xs, xs_words[0], 0, S)
+        load_scales(xs_sc, xs_scales[0])
+        load_w1(0, 1)
+        load_w1(1, 1)
+        for g in range(2):
+            nc.sync.dma_start(
+                out=wl_raw[g][:], in_=wl[g * KP : (g + 1) * KP, :].rearrange("(p j) n -> p j n", j=PACK)
+            )
+        nc.sync.dma_start(
+            out=wc[:].bitcast(I32).rearrange("p (g n) -> p g n", g=2),
+            in_=wc_words.bitcast(I32).rearrange("g p n -> p g n"),
+        )
+        for q in range(QUADS):
+            nc.sync.dma_start(
+                out=wc_sc[rows(q), :].bitcast(I32).rearrange("r (g n) -> r g n", g=2),
+                in_=wc_scales[:, QROWS * q : QROWS * (q + 1), :].bitcast(I32).rearrange("g r n -> r g n"),
+            )
+
+        nc.vector.tensor_copy(
+            out=wg[:].rearrange("p (g t m b) -> p g t m b", g=2, t=PACK, b=2),
+            in_=wg_raw[:].rearrange("p (g m t b) -> p g t m b", g=2, t=PACK, b=2),
+        )
+        nc.vector.tensor_copy(v[0][:], tab[0][:].indirect(offsets[:]))
+        nc.vector.tensor_copy(v_sc[:], tab_sc[:].indirect(offsets[:]))
+        nc.vector.tensor_copy(
+            out=wg_sc[:].rearrange("p (g t m) -> p g t m", g=2, t=PACK),
+            in_=wg_sc_raw[:].rearrange("p (g m t) -> p g t m", g=2, t=PACK),
+        )
+        nc.vector.tensor_copy(v[1][:], tab[1][:].indirect(offsets[:]))
+
+        def round_w1(a, g, m_vec):
+            dst = w1_bf[a, g][:].rearrange("p (t m j) -> p m j t", t=PACK, j=PACK)
+            src = w1_raw[a, g][:].rearrange("p j (m t) -> p m j t", t=PACK)
+            if m_vec > 0:
+                nc.vector.tensor_copy(out=dst[:, :m_vec], in_=src[:, :m_vec])
+            nc.scalar.copy(out=dst[:, m_vec:], in_=src[:, m_vec:])
+
+        def quantise(codes, scales, values, lo, hi):
+            nc.vector.quantize_mx(
+                out=codes[:, lo:hi].bitcast(FP8X4), scales=scales[:, lo:hi], in_=values[:, PACK * lo : PACK * hi]
+            )
+
+        def quantise_w1(a, g, width):
+            for lo in range(0, KP, width):
+                quantise(w1q[a, g], w1_sc[a, g], w1_bf[a, g], lo, lo + width)
+
+        def first_stage(g, c, on_vector=()):
+            cols = slice(c * CHUNK, (c + 1) * CHUNK)
+            h = ring.tile([P, PACK, CHUNK], F32, name="h", bufs=3)
+            for t in range(PACK):
+                acc = acc_pool.tile([P, CHUNK], F32, name="acc")
+                for a in range(2):
+                    nc.tensor.matmul_mx(
+                        out=acc[:],
+                        lhsT=w1q[a, g][:, t * P : (t + 1) * P].bitcast(FP8X4),
+                        lhsT_scale=w1_sc[a, g][:, t * P : (t + 1) * P],
+                        rhs=v[a][:, cols].bitcast(FP8X4),
+                        rhs_scale=v_sc[QROWS * a : P, cols],
+                        start=(a == 0),
+                        stop=(a == 1),
+                    )
+                col = bias[:, g * PACK + t : g * PACK + t + 1]
+                if t in on_vector:
+                    nc.vector.tensor_scalar(h[:, t, :], acc[:], col, 0.0, ALU.add, ALU.max)
+                else:
+                    nc.scalar.activation(h[:, t, :], acc[:], ACT.Relu, bias=col)
+            return h
+
+        def weave(ap):
+            return ap.rearrange("p t (c i) -> p c t i", i=PAIR)
+
+        def woven(ap):
+            return ap.rearrange("p (c i t) -> p c t i", i=PAIR, t=PACK)
+
+        def quantise_h(g, c, h):
+            h_bf = ring.tile([P, PACK * CHUNK], BF16, name="h_bf", align_bytes=64)
+            nc.vector.tensor_copy(out=woven(h_bf[:]), in_=weave(h[:]))
+            quantise(hq[g, c], h_sc[g, c], h_bf, 0, CHUNK)
+
+        def quantise_z(g, c, h, lo, hi):
+            z_bf = ring.tile([P, PACK * CHUNK], BF16, name="z_bf", align_bytes=64)
+            for j in range(lo, hi, BLK):
+                cols = slice(c * CHUNK + j, c * CHUNK + j + BLK)
+                b = b_pool.tile([P, PACK, BLK], F32, name="b")
+                for t in range(PACK):
+                    m = (g * PACK + t) * P
+                    nc.tensor.matmul_mx(
+                        out=b[:, t, :],
+                        lhsT=wg[:, 2 * m : 2 * (m + P)].bitcast(FP4X4),
+                        lhsT_scale=wg_sc[:, m : m + P],
+                        rhs=xs[:, cols].bitcast(FP8X4),
+                        rhs_scale=xs_sc[:, cols],
+                        start=True,
+                        stop=True,
+                    )
+                nc.vector.tensor_tensor(
+                    woven(z_bf[:, PACK * j : PACK * (j + BLK)]), weave(h[:, :, j : j + BLK]), weave(b[:]), ALU.subtract
+                )
+            quantise(zq[g, c], z_sc[g, c], z_bf, lo, hi)
+
+        def damping(c):
+            for n in range(3):
+                acc = acc_pool.tile([P, CHUNK], F32, name="acc")
+                for g in range(2):
+                    m = g * N + n * P
+                    nc.tensor.matmul_mx(
+                        out=acc[:],
+                        lhsT=wc[:, 2 * m : 2 * (m + P)].bitcast(FP4X4),
+                        lhsT_scale=wc_sc[:, m : m + P],
+                        rhs=hq[g, c][:].bitcast(FP8X4),
+                        rhs_scale=h_sc[g, c][:],
+                        start=(g == 0),
+                        stop=(g == 1),
+                    )
+                root = ring.tile([P, CHUNK], F32, name="root")
+                nc.scalar.activation(damp[c, n][:], acc[:], ACT.Abs)
+                nc.scalar.activation(root[:], damp[c, n][:], ACT.Abs_reciprocal_sqrt, bias=1.0)
+                nc.scalar.activation(damp[c, n][:], root[:], ACT.Square)
+
+        def scores(c, lo, hi):
+            for n in range(3):
+                acc = acc_pool.tile([P, CHUNK], F32, name="acc")
+                for g in range(2):
+                    nc.tensor.matmul_mx(
+                        out=acc[:, : hi - lo],
+                        lhsT=wlq[g][:, n * P : (n + 1) * P].bitcast(FP8X4),
+                        lhsT_scale=wl_sc[g][:, n * P : (n + 1) * P],
+                        rhs=zq[g, c][:, lo:hi].bitcast(FP8X4),
+                        rhs_scale=z_sc[g, c][:, lo:hi],
+                        start=(g == 0),
+                        stop=(g == 1),
+                    )
+                res = ring.tile([P, CHUNK], F32, name="res", bufs=6)
+                nc.vector.tensor_tensor(res[:, : hi - lo], acc[:, : hi - lo], damp[c, n][:, lo:hi], ALU.mult)
+                nc.sync.dma_start(
+                    out=out[n * P : (n + 1) * P, c * CHUNK + lo : c * CHUNK + hi], in_=res[:, : hi - lo]
+                )
+
+        def round_wl(g):
+            nc.vector.tensor_copy(out=woven(wl_bf[g][:]), in_=weave(wl_raw[g][:]))
+            quantise(wlq[g], wl_sc[g], wl_bf[g], 0, N)
+
+        round_w1(0, 0, M_VEC)
+        quantise_w1(0, 0, KP)
+        round_w1(1, 0, M_VEC)
+        quantise_w1(1, 0, P)
+
+        h00 = first_stage(0, 0, on_vector=(2, 3))
+        round_w1(0, 1, 0)
+        h01 = first_stage(0, 1)
+        quantise_h(0, 0, h00)
+        quantise_z(0, 0, h00, 0, CHUNK)
+        round_w1(1, 1, 0)
+        quantise_w1(0, 1, KP)
+        quantise_h(0, 1, h01)
+        quantise_w1(1, 1, KP)
+        h10 = first_stage(1, 0)
+        quantise_z(0, 1, h01, 0, CHUNK)
+        h11 = first_stage(1, 1)
+        quantise_h(1, 0, h10)
+        damping(0)
+        round_wl(0)
+        round_wl(1)
+        quantise_z(1, 0, h10, 0, CHUNK)
+        quantise_h(1, 1, h11)
+        damping(1)
+        scores(0, 0, CHUNK)
+        for lo in range(0, CHUNK, CHUNK // 2):
+            quantise_z(1, 1, h11, lo, lo + CHUNK // 2)
+            scores(1, lo, lo + CHUNK // 2)

@@ -24,7 +24,7 @@ QROWS = 4
 CHUNK = 512
 BLK = 128
 PAIR = 2
-M_VEC = 84
+SPREAD = 4
 
 
 def tile_list_handicap_sheet_scores_kernel(
@@ -44,6 +44,7 @@ def tile_list_handicap_sheet_scores_kernel(
         tab = [kept([P, T], U32, "tab%d" % a) for a in range(2)]
         tab_sc = kept([P, T], U8, "tab_sc")
         v = [kept([P, S], U32, "v%d" % a) for a in range(2)]
+        v_sc_rows = kept([P, S], U8, "v_sc_rows")
         v_sc = kept([P, S], U8, "v_sc")
         xs = kept([P, S], U32, "xs")
         xs_sc = kept([P, S], U8, "xs_sc")
@@ -63,14 +64,12 @@ def tile_list_handicap_sheet_scores_kernel(
         wlq = [kept([P, N], U32, "wlq%d" % g) for g in range(2)]
         wl_sc = [kept([P, N], U8, "wl_sc%d" % g) for g in range(2)]
         units = [(g, c) for g in range(2) for c in range(2)]
+        h = {u: kept([P, PACK, CHUNK], F32, "h%d%d" % u) for u in units}
         hq = {u: kept([P, CHUNK], U32, "hq%d%d" % u) for u in units}
         h_sc = {u: kept([P, CHUNK], U8, "h_sc%d%d" % u) for u in units}
         zq = {u: kept([P, CHUNK], U32, "zq%d%d" % u) for u in units}
         z_sc = {u: kept([P, CHUNK], U8, "z_sc%d%d" % u) for u in units}
         damp = {(c, n): kept([P, CHUNK], F32, "damp%d%d" % (c, n)) for c in range(2) for n in range(3)}
-
-        def rows(q, first=0):
-            return slice(32 * q + first, 32 * q + first + QROWS)
 
         def load_words(tile, words, lo, hi):
             nc.sync.dma_start(
@@ -83,30 +82,51 @@ def tile_list_handicap_sheet_scores_kernel(
                 in_=w1[a * KP : (a + 1) * KP, g * KP : (g + 1) * KP].rearrange("(p j) c -> p j c", j=PACK),
             )
 
-        def load_scales(tile, scales, first=0):
-            for q in range(QUADS):
-                nc.sync.dma_start(
-                    out=tile[rows(q, first), :].bitcast(I32), in_=scales[QROWS * q : QROWS * (q + 1), :].bitcast(I32)
-                )
+        def load_scales(queue, tile, scales):
+            for r in range(QROWS):
+                queue.dma_start(out=tile[r:P:32, :].bitcast(I32), in_=scales[r::QROWS, :].bitcast(I32))
 
-        for plane in (tab_sc, wg_sc_raw, xs_sc, wc_sc):
+        def place_scales(rs):
+            for r in rs:
+                for a in range(2):
+                    src = 64 * a + SPREAD * r
+                    nc.sync.dma_start(
+                        out=v_sc[QROWS * a + r : P : 32, :].bitcast(I32),
+                        in_=v_sc_rows[src : src + 49 : 16, :].bitcast(I32),
+                    )
+
+        for plane in (tab_sc, wg_sc_raw, v_sc):
             nc.vector.memset(plane[:].bitcast(I32), 0)
-        nc.sync.dma_start(offsets[:], offs)
-        nc.sync.dma_start(out=wg_raw[:].bitcast(I32), in_=wg_words[0].bitcast(I32))
-        load_words(tab[0], tab_words[0], 0, T // 2)
-        load_scales(tab_sc, tab_scales[0])
-        load_words(tab[0], tab_words[0], T // 2, T)
-        load_scales(tab_sc, tab_scales[1], QROWS)
-        load_words(tab[1], tab_words[1], 0, T // 2)
-        load_scales(wg_sc_raw, wg_scales[0])
-        load_words(tab[1], tab_words[1], T // 2, T)
-        load_w1(0, 0)
-        load_w1(1, 0)
-        nc.sync.dma_start(
+        for plane in (xs_sc, wc_sc):
+            nc.gpsimd.memset(plane[:].bitcast(I32), 0)
+        nc.gpsimd.dma_start(
             out=bias[:].rearrange("p (g t) -> p g t", t=PACK), in_=b1.rearrange("(g p t) -> p g t", g=2, t=PACK)
         )
+        load_scales(nc.gpsimd, xs_sc, xs_scales[0])
+        for r in range(QROWS):
+            nc.gpsimd.dma_start(
+                out=wc_sc[r:P:32, :].bitcast(I32).rearrange("q (g n) -> q g n", g=2),
+                in_=wc_scales[:, r::QROWS, :].bitcast(I32).rearrange("g q n -> q g n"),
+            )
+        nc.sync.dma_start(offsets[:], offs)
+        nc.sync.dma_start(out=wg_raw[:].bitcast(I32), in_=wg_words[0].bitcast(I32))
+        load_w1(0, 0)
+        nc.sync.dma_start(
+            out=tab_sc[0:P:SPREAD, :].bitcast(I32), in_=tab_scales.rearrange("a q n -> (a q) n").bitcast(I32)
+        )
+        load_scales(nc.sync, wg_sc_raw, wg_scales[0])
+        load_words(tab[0], tab_words[0], 0, T)
+        load_words(tab[1], tab_words[1], 0, T // 2)
+        load_words(tab[1], tab_words[1], T // 2, T)
+        nc.vector.tensor_copy(
+            out=wg[:].rearrange("p (g t m b) -> p g t m b", g=2, t=PACK, b=2),
+            in_=wg_raw[:].rearrange("p (g m t b) -> p g t m b", g=2, t=PACK, b=2),
+        )
+        nc.vector.tensor_copy(v_sc_rows[:], tab_sc[:].indirect(offsets[:]))
+        place_scales((0, 1))
+        load_w1(1, 0)
+        place_scales((2, 3))
         load_words(xs, xs_words[0], 0, S)
-        load_scales(xs_sc, xs_scales[0])
         load_w1(0, 1)
         load_w1(1, 1)
         for g in range(2):
@@ -117,23 +137,12 @@ def tile_list_handicap_sheet_scores_kernel(
             out=wc[:].bitcast(I32).rearrange("p (g n) -> p g n", g=2),
             in_=wc_words.bitcast(I32).rearrange("g p n -> p g n"),
         )
-        for q in range(QUADS):
-            nc.sync.dma_start(
-                out=wc_sc[rows(q), :].bitcast(I32).rearrange("r (g n) -> r g n", g=2),
-                in_=wc_scales[:, QROWS * q : QROWS * (q + 1), :].bitcast(I32).rearrange("g r n -> r g n"),
-            )
 
-        nc.vector.tensor_copy(
-            out=wg[:].rearrange("p (g t m b) -> p g t m b", g=2, t=PACK, b=2),
-            in_=wg_raw[:].rearrange("p (g m t b) -> p g t m b", g=2, t=PACK, b=2),
-        )
         nc.vector.tensor_copy(v[0][:], tab[0][:].indirect(offsets[:]))
-        nc.vector.tensor_copy(v_sc[:], tab_sc[:].indirect(offsets[:]))
         nc.vector.tensor_copy(
             out=wg_sc[:].rearrange("p (g t m) -> p g t m", g=2, t=PACK),
             in_=wg_sc_raw[:].rearrange("p (g m t) -> p g t m", g=2, t=PACK),
         )
-        nc.vector.tensor_copy(v[1][:], tab[1][:].indirect(offsets[:]))
 
         def round_w1(a, g, m_vec):
             dst = w1_bf[a, g][:].rearrange("p (t m j) -> p m j t", t=PACK, j=PACK)
@@ -151,14 +160,13 @@ def tile_list_handicap_sheet_scores_kernel(
             for lo in range(0, KP, width):
                 quantise(w1q[a, g], w1_sc[a, g], w1_bf[a, g], lo, lo + width)
 
-        def first_stage(g, c, on_vector=()):
-            cols = slice(c * CHUNK, (c + 1) * CHUNK)
-            h = ring.tile([P, PACK, CHUNK], F32, name="h", bufs=3)
+        def first_stage(g, c, lo=0, hi=CHUNK, on_vector=()):
+            cols = slice(c * CHUNK + lo, c * CHUNK + hi)
             for t in range(PACK):
                 acc = acc_pool.tile([P, CHUNK], F32, name="acc")
                 for a in range(2):
                     nc.tensor.matmul_mx(
-                        out=acc[:],
+                        out=acc[:, : hi - lo],
                         lhsT=w1q[a, g][:, t * P : (t + 1) * P].bitcast(FP8X4),
                         lhsT_scale=w1_sc[a, g][:, t * P : (t + 1) * P],
                         rhs=v[a][:, cols].bitcast(FP8X4),
@@ -168,10 +176,9 @@ def tile_list_handicap_sheet_scores_kernel(
                     )
                 col = bias[:, g * PACK + t : g * PACK + t + 1]
                 if t in on_vector:
-                    nc.vector.tensor_scalar(h[:, t, :], acc[:], col, 0.0, ALU.add, ALU.max)
+                    nc.vector.tensor_scalar(h[g, c][:, t, lo:hi], acc[:, : hi - lo], col, 0.0, ALU.add, ALU.max)
                 else:
-                    nc.scalar.activation(h[:, t, :], acc[:], ACT.Relu, bias=col)
-            return h
+                    nc.scalar.activation(h[g, c][:, t, lo:hi], acc[:, : hi - lo], ACT.Relu, bias=col)
 
         def weave(ap):
             return ap.rearrange("p t (c i) -> p c t i", i=PAIR)
@@ -179,12 +186,12 @@ def tile_list_handicap_sheet_scores_kernel(
         def woven(ap):
             return ap.rearrange("p (c i t) -> p c t i", i=PAIR, t=PACK)
 
-        def quantise_h(g, c, h):
+        def quantise_h(g, c, lo=0, hi=CHUNK):
             h_bf = ring.tile([P, PACK * CHUNK], BF16, name="h_bf", align_bytes=64)
-            nc.vector.tensor_copy(out=woven(h_bf[:]), in_=weave(h[:]))
-            quantise(hq[g, c], h_sc[g, c], h_bf, 0, CHUNK)
+            nc.vector.tensor_copy(out=woven(h_bf[:, PACK * lo : PACK * hi]), in_=weave(h[g, c][:, :, lo:hi]))
+            quantise(hq[g, c], h_sc[g, c], h_bf, lo, hi)
 
-        def quantise_z(g, c, h, lo, hi):
+        def quantise_z(g, c, lo=0, hi=CHUNK):
             z_bf = ring.tile([P, PACK * CHUNK], BF16, name="z_bf", align_bytes=64)
             for j in range(lo, hi, BLK):
                 cols = slice(c * CHUNK + j, c * CHUNK + j + BLK)
@@ -201,7 +208,7 @@ def tile_list_handicap_sheet_scores_kernel(
                         stop=True,
                     )
                 nc.vector.tensor_tensor(
-                    woven(z_bf[:, PACK * j : PACK * (j + BLK)]), weave(h[:, :, j : j + BLK]), weave(b[:]), ALU.subtract
+                    woven(z_bf[:, PACK * j : PACK * (j + BLK)]), weave(h[g, c][:, :, j : j + BLK]), weave(b[:]), ALU.subtract
                 )
             quantise(zq[g, c], z_sc[g, c], z_bf, lo, hi)
 
@@ -243,35 +250,40 @@ def tile_list_handicap_sheet_scores_kernel(
                     out=out[n * P : (n + 1) * P, c * CHUNK + lo : c * CHUNK + hi], in_=res[:, : hi - lo]
                 )
 
-        def round_wl(g):
-            nc.vector.tensor_copy(out=woven(wl_bf[g][:]), in_=weave(wl_raw[g][:]))
+        def round_wl(g, copy):
+            copy(out=woven(wl_bf[g][:]), in_=weave(wl_raw[g][:]))
             quantise(wlq[g], wl_sc[g], wl_bf[g], 0, N)
 
-        round_w1(0, 0, M_VEC)
+        round_w1(0, 0, 0)
         quantise_w1(0, 0, KP)
-        round_w1(1, 0, M_VEC)
+        nc.vector.tensor_copy(v[1][:], tab[1][:].indirect(offsets[:]))
+        round_w1(1, 0, 80)
         quantise_w1(1, 0, P)
 
-        h00 = first_stage(0, 0, on_vector=(2, 3))
+        HALF = CHUNK // 2
+        first_stage(0, 0, 0, HALF, on_vector=(2, 3))
+        first_stage(0, 0, HALF, CHUNK)
+        first_stage(0, 1)
         round_w1(0, 1, 0)
-        h01 = first_stage(0, 1)
-        quantise_h(0, 0, h00)
-        quantise_z(0, 0, h00, 0, CHUNK)
-        round_w1(1, 1, 0)
         quantise_w1(0, 1, KP)
-        quantise_h(0, 1, h01)
+        round_w1(1, 1, 0)
         quantise_w1(1, 1, KP)
-        h10 = first_stage(1, 0)
-        quantise_z(0, 1, h01, 0, CHUNK)
-        h11 = first_stage(1, 1)
-        quantise_h(1, 0, h10)
+        quantise_h(0, 0, 0, HALF)
+        quantise_h(0, 0, HALF, CHUNK)
+        quantise_h(0, 1)
+        quantise_z(0, 0)
+        quantise_z(0, 1)
+        first_stage(1, 0)
+        first_stage(1, 1)
+        quantise_h(1, 0)
+        quantise_h(1, 1)
         damping(0)
-        round_wl(0)
-        round_wl(1)
-        quantise_z(1, 0, h10, 0, CHUNK)
-        quantise_h(1, 1, h11)
+        round_wl(0, nc.vector.tensor_copy)
+        round_wl(1, nc.scalar.copy)
         damping(1)
+        quantise_z(1, 0)
+        quantise_z(1, 1, 0, HALF)
         scores(0, 0, CHUNK)
-        for lo in range(0, CHUNK, CHUNK // 2):
-            quantise_z(1, 1, h11, lo, lo + CHUNK // 2)
-            scores(1, lo, lo + CHUNK // 2)
+        quantise_z(1, 1, HALF, CHUNK)
+        scores(1, 0, HALF)
+        scores(1, HALF, CHUNK)

@@ -25,6 +25,9 @@ CHUNK = 512
 BLK = 128
 PAIR = 2
 SPREAD = 4
+ACC_BANKS = 6
+B_BANKS = 2
+HALF = CHUNK // 2
 
 
 def tile_list_handicap_sheet_scores_kernel(
@@ -34,8 +37,13 @@ def tile_list_handicap_sheet_scores_kernel(
     with ExitStack() as ctx:
         keep = ctx.enter_context(tc.tile_pool(name="keep", bufs=1))
         ring = ctx.enter_context(tc.tile_pool(name="ring", bufs=2))
-        acc_pool = ctx.enter_context(tc.psum_pool(name="acc", bufs=6))
-        b_pool = ctx.enter_context(tc.psum_pool(name="bsum", bufs=2))
+        psum = ctx.enter_context(tc.psum_pool(name="psum", bufs=1))
+        acc_tiles = []
+        b_tiles = {}
+
+        def acc_bank():
+            acc_tiles.append(psum.tile([P, CHUNK], F32, name="acc%d" % (len(acc_tiles) % ACC_BANKS)))
+            return acc_tiles[-1]
 
         def kept(shape, dtype, name):
             return keep.tile(shape, dtype, name=name, align_bytes=64)
@@ -95,6 +103,10 @@ def tile_list_handicap_sheet_scores_kernel(
                         in_=v_sc_rows[src : src + 49 : 16, :].bitcast(I32),
                     )
 
+        warm_in = kept([P, 1], F32, "warm_in")
+        warm_out = kept([P, 1], F32, "warm_out")
+        nc.gpsimd.memset(warm_in[:], 1.0)
+        nc.scalar.activation(warm_out[:], warm_in[:], ACT.Abs_reciprocal_sqrt)
         for plane in (tab_sc, wg_sc_raw, v_sc):
             nc.vector.memset(plane[:].bitcast(I32), 0)
         for plane in (xs_sc, wc_sc):
@@ -163,7 +175,7 @@ def tile_list_handicap_sheet_scores_kernel(
         def first_stage(g, c, lo=0, hi=CHUNK, on_vector=()):
             cols = slice(c * CHUNK + lo, c * CHUNK + hi)
             for t in range(PACK):
-                acc = acc_pool.tile([P, CHUNK], F32, name="acc")
+                acc = acc_bank()
                 for a in range(2):
                     nc.tensor.matmul_mx(
                         out=acc[:, : hi - lo],
@@ -191,11 +203,11 @@ def tile_list_handicap_sheet_scores_kernel(
             nc.vector.tensor_copy(out=woven(h_bf[:, PACK * lo : PACK * hi]), in_=weave(h[g, c][:, :, lo:hi]))
             quantise(hq[g, c], h_sc[g, c], h_bf, lo, hi)
 
-        def quantise_z(g, c, lo=0, hi=CHUNK):
-            z_bf = ring.tile([P, PACK * CHUNK], BF16, name="z_bf", align_bytes=64)
-            for j in range(lo, hi, BLK):
+        def stream_product(g, c):
+            for j in range(0, CHUNK, BLK):
                 cols = slice(c * CHUNK + j, c * CHUNK + j + BLK)
-                b = b_pool.tile([P, PACK, BLK], F32, name="b")
+                b = psum.tile([P, PACK, BLK], F32, name="b%d" % (len(b_tiles) % B_BANKS))
+                b_tiles[g, c, j] = b
                 for t in range(PACK):
                     m = (g * PACK + t) * P
                     nc.tensor.matmul_mx(
@@ -207,14 +219,21 @@ def tile_list_handicap_sheet_scores_kernel(
                         start=True,
                         stop=True,
                     )
+
+        def quantise_z(g, c, lo=0, hi=CHUNK):
+            z_bf = ring.tile([P, PACK * CHUNK], BF16, name="z_bf", align_bytes=64)
+            for j in range(lo, hi, BLK):
                 nc.vector.tensor_tensor(
-                    woven(z_bf[:, PACK * j : PACK * (j + BLK)]), weave(h[g, c][:, :, j : j + BLK]), weave(b[:]), ALU.subtract
+                    woven(z_bf[:, PACK * j : PACK * (j + BLK)]),
+                    weave(h[g, c][:, :, j : j + BLK]),
+                    weave(b_tiles[g, c, j][:]),
+                    ALU.subtract,
                 )
             quantise(zq[g, c], z_sc[g, c], z_bf, lo, hi)
 
         def damping(c):
             for n in range(3):
-                acc = acc_pool.tile([P, CHUNK], F32, name="acc")
+                acc = acc_bank()
                 for g in range(2):
                     m = g * N + n * P
                     nc.tensor.matmul_mx(
@@ -233,7 +252,7 @@ def tile_list_handicap_sheet_scores_kernel(
 
         def scores(c, lo, hi):
             for n in range(3):
-                acc = acc_pool.tile([P, CHUNK], F32, name="acc")
+                acc = acc_bank()
                 for g in range(2):
                     nc.tensor.matmul_mx(
                         out=acc[:, : hi - lo],
@@ -251,7 +270,8 @@ def tile_list_handicap_sheet_scores_kernel(
                 )
 
         def round_wl(g, copy):
-            copy(out=woven(wl_bf[g][:]), in_=weave(wl_raw[g][:]))
+            for n in range(0, N, P):
+                copy(out=woven(wl_bf[g][:, PACK * n : PACK * (n + P)]), in_=weave(wl_raw[g][:, :, n : n + P]))
             quantise(wlq[g], wl_sc[g], wl_bf[g], 0, N)
 
         round_w1(0, 0, 0)
@@ -260,30 +280,31 @@ def tile_list_handicap_sheet_scores_kernel(
         round_w1(1, 0, 80)
         quantise_w1(1, 0, P)
 
-        HALF = CHUNK // 2
         first_stage(0, 0, 0, HALF, on_vector=(2, 3))
         first_stage(0, 0, HALF, CHUNK)
+        for g, c in units:
+            stream_product(g, c)
         first_stage(0, 1)
-        round_w1(0, 1, 0)
+        round_w1(0, 1, 32)
         quantise_w1(0, 1, KP)
         round_w1(1, 1, 0)
         quantise_w1(1, 1, KP)
+        first_stage(1, 0)
+        first_stage(1, 1)
         quantise_h(0, 0, 0, HALF)
         quantise_h(0, 0, HALF, CHUNK)
         quantise_h(0, 1)
-        quantise_z(0, 0)
-        quantise_z(0, 1)
-        first_stage(1, 0)
-        first_stage(1, 1)
         quantise_h(1, 0)
         quantise_h(1, 1)
-        damping(0)
-        round_wl(0, nc.vector.tensor_copy)
+        round_wl(0, nc.scalar.copy)
         round_wl(1, nc.scalar.copy)
+        damping(0)
         damping(1)
+        quantise_z(0, 0)
+        quantise_z(0, 1)
         quantise_z(1, 0)
-        quantise_z(1, 1, 0, HALF)
         scores(0, 0, CHUNK)
-        quantise_z(1, 1, HALF, CHUNK)
+        quantise_z(1, 1, 0, HALF)
         scores(1, 0, HALF)
+        quantise_z(1, 1, HALF, CHUNK)
         scores(1, HALF, CHUNK)

@@ -19,15 +19,22 @@ ACT = mybir.ActivationFunctionType
 P = 128
 PACK = 4
 KP = P * PACK
-QUADS = 4
+PASSES = K // KP
+GROUPS = H // KP
+N_TILES = N // P
+QUAD = 32
 QROWS = 4
+FP4_BYTES = 2
+LIST_ROWS = 16
 CHUNK = 512
+CHUNKS = S // CHUNK
+HALF = CHUNK // 2
 BLK = 128
 PAIR = 2
 SPREAD = 4
-ACC_BANKS = 6
-B_BANKS = 2
-HALF = CHUNK // 2
+ACC_BANKS = 5
+B_BANKS = 3
+W1_ON_VECTOR = {(0, 0): 0, (1, 0): 80, (0, 1): P, (1, 1): 0}
 
 
 def tile_list_handicap_sheet_scores_kernel(
@@ -48,36 +55,37 @@ def tile_list_handicap_sheet_scores_kernel(
         def kept(shape, dtype, name):
             return keep.tile(shape, dtype, name=name, align_bytes=64)
 
-        offsets = keep.tile([P, S // 16], U16, name="offsets")
-        tab = [kept([P, T], U32, "tab%d" % a) for a in range(2)]
+        pieces = [(a, g) for g in range(GROUPS) for a in range(PASSES)]
+        units = [(g, c) for g in range(GROUPS) for c in range(CHUNKS)]
+        offsets = keep.tile([P, S // LIST_ROWS], U16, name="offsets")
+        tab = [kept([P, T], U32, "tab%d" % a) for a in range(PASSES)]
         tab_sc = kept([P, T], U8, "tab_sc")
-        v = [kept([P, S], U32, "v%d" % a) for a in range(2)]
+        v = [kept([P, S], U32, "v%d" % a) for a in range(PASSES)]
         v_sc_rows = kept([P, S], U8, "v_sc_rows")
         v_sc = kept([P, S], U8, "v_sc")
         xs = kept([P, S], U32, "xs")
         xs_sc = kept([P, S], U8, "xs_sc")
-        wg_raw = kept([P, 2 * H], U8, "wg_raw")
+        wg_raw = kept([P, FP4_BYTES * H], U8, "wg_raw")
         wg_sc_raw = kept([P, H], U8, "wg_sc_raw")
-        wg = kept([P, 2 * H], U8, "wg")
+        wg = kept([P, FP4_BYTES * H], U8, "wg")
         wg_sc = kept([P, H], U8, "wg_sc")
-        wc = kept([P, 2 * 2 * N], U8, "wc")
-        wc_sc = kept([P, 2 * N], U8, "wc_sc")
-        bias = kept([P, 2 * PACK], F32, "bias")
-        w1_raw = {(a, g): kept([P, PACK, KP], F32, "w1_raw%d%d" % (a, g)) for g in range(2) for a in range(2)}
-        w1_bf = {(a, g): kept([P, PACK * KP], BF16, "w1_bf%d%d" % (a, g)) for g in range(2) for a in range(2)}
-        w1q = {(a, g): kept([P, KP], U32, "w1q%d%d" % (a, g)) for g in range(2) for a in range(2)}
-        w1_sc = {(a, g): kept([P, KP], U8, "w1_sc%d%d" % (a, g)) for g in range(2) for a in range(2)}
-        wl_raw = [kept([P, PACK, N], F32, "wl_raw%d" % g) for g in range(2)]
-        wl_bf = [kept([P, PACK * N], BF16, "wl_bf%d" % g) for g in range(2)]
-        wlq = [kept([P, N], U32, "wlq%d" % g) for g in range(2)]
-        wl_sc = [kept([P, N], U8, "wl_sc%d" % g) for g in range(2)]
-        units = [(g, c) for g in range(2) for c in range(2)]
-        h = {u: kept([P, PACK, CHUNK], F32, "h%d%d" % u) for u in units}
-        hq = {u: kept([P, CHUNK], U32, "hq%d%d" % u) for u in units}
-        h_sc = {u: kept([P, CHUNK], U8, "h_sc%d%d" % u) for u in units}
-        zq = {u: kept([P, CHUNK], U32, "zq%d%d" % u) for u in units}
-        z_sc = {u: kept([P, CHUNK], U8, "z_sc%d%d" % u) for u in units}
-        damp = {(c, n): kept([P, CHUNK], F32, "damp%d%d" % (c, n)) for c in range(2) for n in range(3)}
+        wc = kept([P, GROUPS * FP4_BYTES * N], U8, "wc")
+        wc_sc = kept([P, GROUPS * N], U8, "wc_sc")
+        bias = kept([P, GROUPS * PACK], F32, "bias")
+        w1_raw = {piece: kept([P, PACK, KP], F32, "w1_raw%d%d" % piece) for piece in pieces}
+        w1_bf = {piece: kept([P, PACK * KP], BF16, "w1_bf%d%d" % piece) for piece in pieces}
+        w1q = {piece: kept([P, KP], U32, "w1q%d%d" % piece) for piece in pieces}
+        w1_sc = {piece: kept([P, KP], U8, "w1_sc%d%d" % piece) for piece in pieces}
+        wl_raw = [kept([P, PACK, N], F32, "wl_raw%d" % g) for g in range(GROUPS)]
+        wl_bf = [kept([P, PACK * N], BF16, "wl_bf%d" % g) for g in range(GROUPS)]
+        wlq = [kept([P, N], U32, "wlq%d" % g) for g in range(GROUPS)]
+        wl_sc = [kept([P, N], U8, "wl_sc%d" % g) for g in range(GROUPS)]
+        h = {unit: kept([P, PACK, CHUNK], F32, "h%d%d" % unit) for unit in units}
+        hq = {unit: kept([P, CHUNK], U32, "hq%d%d" % unit) for unit in units}
+        h_sc = {unit: kept([P, CHUNK], U8, "h_sc%d%d" % unit) for unit in units}
+        zq = {unit: kept([P, CHUNK], U32, "zq%d%d" % unit) for unit in units}
+        z_sc = {unit: kept([P, CHUNK], U8, "z_sc%d%d" % unit) for unit in units}
+        damp = {(c, n): kept([P, CHUNK], F32, "damp%d%d" % (c, n)) for c in range(CHUNKS) for n in range(N_TILES)}
 
         def load_words(tile, words, lo, hi):
             nc.sync.dma_start(
@@ -92,34 +100,38 @@ def tile_list_handicap_sheet_scores_kernel(
 
         def load_scales(queue, tile, scales):
             for r in range(QROWS):
-                queue.dma_start(out=tile[r:P:32, :].bitcast(I32), in_=scales[r::QROWS, :].bitcast(I32))
+                queue.dma_start(out=tile[r:P:QUAD, :].bitcast(I32), in_=scales[r::QROWS, :].bitcast(I32))
 
         def place_scales(rs):
+            step = SPREAD * QROWS
             for r in rs:
-                for a in range(2):
-                    src = 64 * a + SPREAD * r
+                for a in range(PASSES):
+                    first = SPREAD * (QROWS * QROWS * a + r)
                     nc.sync.dma_start(
-                        out=v_sc[QROWS * a + r : P : 32, :].bitcast(I32),
-                        in_=v_sc_rows[src : src + 49 : 16, :].bitcast(I32),
+                        out=v_sc[QROWS * a + r : P : QUAD, :].bitcast(I32),
+                        in_=v_sc_rows[first : first + (QROWS - 1) * step + 1 : step, :].bitcast(I32),
                     )
 
         warm_in = kept([P, 1], F32, "warm_in")
         warm_out = kept([P, 1], F32, "warm_out")
         nc.gpsimd.memset(warm_in[:], 1.0)
         nc.scalar.activation(warm_out[:], warm_in[:], ACT.Abs_reciprocal_sqrt)
-        for plane in (tab_sc, wg_sc_raw, v_sc):
-            nc.vector.memset(plane[:].bitcast(I32), 0)
-        for plane in (xs_sc, wc_sc):
-            nc.gpsimd.memset(plane[:].bitcast(I32), 0)
+
+        for scale_tile in (tab_sc, wg_sc_raw, v_sc):
+            nc.vector.memset(scale_tile[:].bitcast(I32), 0)
+        for scale_tile in (xs_sc, wc_sc):
+            nc.gpsimd.memset(scale_tile[:].bitcast(I32), 0)
+
         nc.gpsimd.dma_start(
-            out=bias[:].rearrange("p (g t) -> p g t", t=PACK), in_=b1.rearrange("(g p t) -> p g t", g=2, t=PACK)
+            out=bias[:].rearrange("p (g t) -> p g t", t=PACK), in_=b1.rearrange("(g p t) -> p g t", g=GROUPS, t=PACK)
         )
         load_scales(nc.gpsimd, xs_sc, xs_scales[0])
         for r in range(QROWS):
             nc.gpsimd.dma_start(
-                out=wc_sc[r:P:32, :].bitcast(I32).rearrange("q (g n) -> q g n", g=2),
+                out=wc_sc[r:P:QUAD, :].bitcast(I32).rearrange("q (g n) -> q g n", g=GROUPS),
                 in_=wc_scales[:, r::QROWS, :].bitcast(I32).rearrange("g q n -> q g n"),
             )
+
         nc.sync.dma_start(offsets[:], offs)
         nc.sync.dma_start(out=wg_raw[:].bitcast(I32), in_=wg_words[0].bitcast(I32))
         load_w1(0, 0)
@@ -131,37 +143,30 @@ def tile_list_handicap_sheet_scores_kernel(
         load_words(tab[1], tab_words[1], 0, T // 2)
         load_words(tab[1], tab_words[1], T // 2, T)
         nc.vector.tensor_copy(
-            out=wg[:].rearrange("p (g t m b) -> p g t m b", g=2, t=PACK, b=2),
-            in_=wg_raw[:].rearrange("p (g m t b) -> p g t m b", g=2, t=PACK, b=2),
+            out=wg[:].rearrange("p (g t m b) -> p g t m b", g=GROUPS, t=PACK, b=FP4_BYTES),
+            in_=wg_raw[:].rearrange("p (g m t b) -> p g t m b", g=GROUPS, t=PACK, b=FP4_BYTES),
         )
         nc.vector.tensor_copy(v_sc_rows[:], tab_sc[:].indirect(offsets[:]))
-        place_scales((0, 1))
+        place_scales(range(0, QROWS // 2))
         load_w1(1, 0)
-        place_scales((2, 3))
+        place_scales(range(QROWS // 2, QROWS))
         load_words(xs, xs_words[0], 0, S)
         load_w1(0, 1)
         load_w1(1, 1)
-        for g in range(2):
+        for g in range(GROUPS):
             nc.sync.dma_start(
                 out=wl_raw[g][:], in_=wl[g * KP : (g + 1) * KP, :].rearrange("(p j) n -> p j n", j=PACK)
             )
         nc.sync.dma_start(
-            out=wc[:].bitcast(I32).rearrange("p (g n) -> p g n", g=2),
+            out=wc[:].bitcast(I32).rearrange("p (g n) -> p g n", g=GROUPS),
             in_=wc_words.bitcast(I32).rearrange("g p n -> p g n"),
         )
 
         nc.vector.tensor_copy(v[0][:], tab[0][:].indirect(offsets[:]))
         nc.vector.tensor_copy(
-            out=wg_sc[:].rearrange("p (g t m) -> p g t m", g=2, t=PACK),
-            in_=wg_sc_raw[:].rearrange("p (g m t) -> p g t m", g=2, t=PACK),
+            out=wg_sc[:].rearrange("p (g t m) -> p g t m", g=GROUPS, t=PACK),
+            in_=wg_sc_raw[:].rearrange("p (g m t) -> p g t m", g=GROUPS, t=PACK),
         )
-
-        def round_w1(a, g, m_vec):
-            dst = w1_bf[a, g][:].rearrange("p (t m j) -> p m j t", t=PACK, j=PACK)
-            src = w1_raw[a, g][:].rearrange("p j (m t) -> p m j t", t=PACK)
-            if m_vec > 0:
-                nc.vector.tensor_copy(out=dst[:, :m_vec], in_=src[:, :m_vec])
-            nc.scalar.copy(out=dst[:, m_vec:], in_=src[:, m_vec:])
 
         def quantise(codes, scales, values, lo, hi):
             nc.vector.quantize_mx(
@@ -169,6 +174,13 @@ def tile_list_handicap_sheet_scores_kernel(
             )
 
         def quantise_w1(a, g, width):
+            dst = w1_bf[a, g][:].rearrange("p (t m j) -> p m j t", t=PACK, j=PACK)
+            src = w1_raw[a, g][:].rearrange("p j (m t) -> p m j t", t=PACK)
+            share = W1_ON_VECTOR[a, g]
+            if share > 0:
+                nc.vector.tensor_copy(out=dst[:, :share], in_=src[:, :share])
+            if share < P:
+                nc.scalar.copy(out=dst[:, share:], in_=src[:, share:])
             for lo in range(0, KP, width):
                 quantise(w1q[a, g], w1_sc[a, g], w1_bf[a, g], lo, lo + width)
 
@@ -176,7 +188,7 @@ def tile_list_handicap_sheet_scores_kernel(
             cols = slice(c * CHUNK + lo, c * CHUNK + hi)
             for t in range(PACK):
                 acc = acc_bank()
-                for a in range(2):
+                for a in range(PASSES):
                     nc.tensor.matmul_mx(
                         out=acc[:, : hi - lo],
                         lhsT=w1q[a, g][:, t * P : (t + 1) * P].bitcast(FP8X4),
@@ -184,15 +196,15 @@ def tile_list_handicap_sheet_scores_kernel(
                         rhs=v[a][:, cols].bitcast(FP8X4),
                         rhs_scale=v_sc[QROWS * a : P, cols],
                         start=(a == 0),
-                        stop=(a == 1),
+                        stop=(a == PASSES - 1),
                     )
-                col = bias[:, g * PACK + t : g * PACK + t + 1]
+                b1_rows = bias[:, g * PACK + t : g * PACK + t + 1]
                 if t in on_vector:
-                    nc.vector.tensor_scalar(h[g, c][:, t, lo:hi], acc[:, : hi - lo], col, 0.0, ALU.add, ALU.max)
+                    nc.vector.tensor_scalar(h[g, c][:, t, lo:hi], acc[:, : hi - lo], b1_rows, 0.0, ALU.add, ALU.max)
                 else:
-                    nc.scalar.activation(h[g, c][:, t, lo:hi], acc[:, : hi - lo], ACT.Relu, bias=col)
+                    nc.scalar.activation(h[g, c][:, t, lo:hi], acc[:, : hi - lo], ACT.Relu, bias=b1_rows)
 
-        def weave(ap):
+        def by_rows(ap):
             return ap.rearrange("p t (c i) -> p c t i", i=PAIR)
 
         def woven(ap):
@@ -200,7 +212,7 @@ def tile_list_handicap_sheet_scores_kernel(
 
         def quantise_h(g, c, lo=0, hi=CHUNK):
             h_bf = ring.tile([P, PACK * CHUNK], BF16, name="h_bf", align_bytes=64)
-            nc.vector.tensor_copy(out=woven(h_bf[:, PACK * lo : PACK * hi]), in_=weave(h[g, c][:, :, lo:hi]))
+            nc.vector.tensor_copy(out=woven(h_bf[:, PACK * lo : PACK * hi]), in_=by_rows(h[g, c][:, :, lo:hi]))
             quantise(hq[g, c], h_sc[g, c], h_bf, lo, hi)
 
         def stream_product(g, c):
@@ -209,11 +221,11 @@ def tile_list_handicap_sheet_scores_kernel(
                 b = psum.tile([P, PACK, BLK], F32, name="b%d" % (len(b_tiles) % B_BANKS))
                 b_tiles[g, c, j] = b
                 for t in range(PACK):
-                    m = (g * PACK + t) * P
+                    place = (g * PACK + t) * P
                     nc.tensor.matmul_mx(
                         out=b[:, t, :],
-                        lhsT=wg[:, 2 * m : 2 * (m + P)].bitcast(FP4X4),
-                        lhsT_scale=wg_sc[:, m : m + P],
+                        lhsT=wg[:, FP4_BYTES * place : FP4_BYTES * (place + P)].bitcast(FP4X4),
+                        lhsT_scale=wg_sc[:, place : place + P],
                         rhs=xs[:, cols].bitcast(FP8X4),
                         rhs_scale=xs_sc[:, cols],
                         start=True,
@@ -225,35 +237,35 @@ def tile_list_handicap_sheet_scores_kernel(
             for j in range(lo, hi, BLK):
                 nc.vector.tensor_tensor(
                     woven(z_bf[:, PACK * j : PACK * (j + BLK)]),
-                    weave(h[g, c][:, :, j : j + BLK]),
-                    weave(b_tiles[g, c, j][:]),
+                    by_rows(h[g, c][:, :, j : j + BLK]),
+                    by_rows(b_tiles[g, c, j][:]),
                     ALU.subtract,
                 )
             quantise(zq[g, c], z_sc[g, c], z_bf, lo, hi)
 
         def damping(c):
-            for n in range(3):
+            for n in range(N_TILES):
                 acc = acc_bank()
-                for g in range(2):
-                    m = g * N + n * P
+                for g in range(GROUPS):
+                    col = g * N + n * P
                     nc.tensor.matmul_mx(
                         out=acc[:],
-                        lhsT=wc[:, 2 * m : 2 * (m + P)].bitcast(FP4X4),
-                        lhsT_scale=wc_sc[:, m : m + P],
+                        lhsT=wc[:, FP4_BYTES * col : FP4_BYTES * (col + P)].bitcast(FP4X4),
+                        lhsT_scale=wc_sc[:, col : col + P],
                         rhs=hq[g, c][:].bitcast(FP8X4),
                         rhs_scale=h_sc[g, c][:],
                         start=(g == 0),
-                        stop=(g == 1),
+                        stop=(g == GROUPS - 1),
                     )
                 root = ring.tile([P, CHUNK], F32, name="root")
                 nc.scalar.activation(damp[c, n][:], acc[:], ACT.Abs)
                 nc.scalar.activation(root[:], damp[c, n][:], ACT.Abs_reciprocal_sqrt, bias=1.0)
                 nc.scalar.activation(damp[c, n][:], root[:], ACT.Square)
 
-        def scores(c, lo, hi):
-            for n in range(3):
+        def scores(c, lo=0, hi=CHUNK):
+            for n in range(N_TILES):
                 acc = acc_bank()
-                for g in range(2):
+                for g in range(GROUPS):
                     nc.tensor.matmul_mx(
                         out=acc[:, : hi - lo],
                         lhsT=wlq[g][:, n * P : (n + 1) * P].bitcast(FP8X4),
@@ -261,33 +273,30 @@ def tile_list_handicap_sheet_scores_kernel(
                         rhs=zq[g, c][:, lo:hi].bitcast(FP8X4),
                         rhs_scale=z_sc[g, c][:, lo:hi],
                         start=(g == 0),
-                        stop=(g == 1),
+                        stop=(g == GROUPS - 1),
                     )
-                res = ring.tile([P, CHUNK], F32, name="res", bufs=6)
+                res = ring.tile([P, CHUNK], F32, name="res", bufs=2 * N_TILES)
                 nc.vector.tensor_tensor(res[:, : hi - lo], acc[:, : hi - lo], damp[c, n][:, lo:hi], ALU.mult)
                 nc.sync.dma_start(
                     out=out[n * P : (n + 1) * P, c * CHUNK + lo : c * CHUNK + hi], in_=res[:, : hi - lo]
                 )
 
-        def round_wl(g, copy):
+        def quantise_wl(g):
             for n in range(0, N, P):
-                copy(out=woven(wl_bf[g][:, PACK * n : PACK * (n + P)]), in_=weave(wl_raw[g][:, :, n : n + P]))
+                nc.scalar.copy(
+                    out=woven(wl_bf[g][:, PACK * n : PACK * (n + P)]), in_=by_rows(wl_raw[g][:, :, n : n + P])
+                )
             quantise(wlq[g], wl_sc[g], wl_bf[g], 0, N)
 
-        round_w1(0, 0, 0)
         quantise_w1(0, 0, KP)
         nc.vector.tensor_copy(v[1][:], tab[1][:].indirect(offsets[:]))
-        round_w1(1, 0, 80)
         quantise_w1(1, 0, P)
-
         first_stage(0, 0, 0, HALF, on_vector=(2, 3))
         first_stage(0, 0, HALF, CHUNK)
         for g, c in units:
             stream_product(g, c)
         first_stage(0, 1)
-        round_w1(0, 1, 32)
         quantise_w1(0, 1, KP)
-        round_w1(1, 1, 0)
         quantise_w1(1, 1, KP)
         first_stage(1, 0)
         first_stage(1, 1)
@@ -296,15 +305,15 @@ def tile_list_handicap_sheet_scores_kernel(
         quantise_h(0, 1)
         quantise_h(1, 0)
         quantise_h(1, 1)
-        round_wl(0, nc.scalar.copy)
-        round_wl(1, nc.scalar.copy)
+        quantise_wl(0)
+        quantise_wl(1)
         damping(0)
         damping(1)
         quantise_z(0, 0)
         quantise_z(0, 1)
         quantise_z(1, 0)
-        scores(0, 0, CHUNK)
+        scores(0)
         quantise_z(1, 1, 0, HALF)
-        scores(1, 0, HALF)
         quantise_z(1, 1, HALF, CHUNK)
+        scores(1, 0, HALF)
         scores(1, HALF, CHUNK)

from contextlib import ExitStack

import concourse.mybir as mybir

K, K2, T, S, H, N = 1024, 512, 4096, 1024, 1024, 384
FLOPS = 2 * S * (K * H + K2 * H + 2 * H * N)

F32 = mybir.dt.float32
BF16 = mybir.dt.bfloat16
I32 = mybir.dt.int32
U32 = mybir.dt.uint32
U16 = mybir.dt.uint16
U8 = mybir.dt.uint8
FP8X4 = mybir.dt.float8_e4m3fn_x4
FP4X4 = mybir.dt.float4_e2m1fn_x4
ALU = mybir.AluOpType
ACT = mybir.ActivationFunctionType

P = 128
PACK = 4
KP = P * PACK
PASSES = K // KP
GROUPS = H // KP
N_TILES = N // P
QUAD = 32
QROWS = 4
FP4_BYTES = 2
LIST_ROWS = 16
CHUNK = 512
CHUNKS = S // CHUNK
HALF = CHUNK // 2
BLK = 128
PAIR = 2
SPREAD = 4
ACC_BANKS = 5
B_BANKS = 3
W1_ON_VECTOR = {(0, 0): 0, (1, 0): 80, (0, 1): P, (1, 1): 0}


def tile_list_handicap_sheet_scores_kernel(
    tc, tab_words, tab_scales, offs, xs_words, xs_scales, w1, b1, wg_words, wg_scales, wl, wc_words, wc_scales, out
):
    nc = tc.nc
    with ExitStack() as ctx:
        keep = ctx.enter_context(tc.tile_pool(name="keep", bufs=1))
        ring = ctx.enter_context(tc.tile_pool(name="ring", bufs=2))
        psum = ctx.enter_context(tc.psum_pool(name="psum", bufs=1))
        acc_tiles = []
        b_tiles = {}

        def acc_bank():
            acc_tiles.append(psum.tile([P, CHUNK], F32, name="acc%d" % (len(acc_tiles) % ACC_BANKS)))
            return acc_tiles[-1]

        def kept(shape, dtype, name):
            return keep.tile(shape, dtype, name=name, align_bytes=64)

        pieces = [(a, g) for g in range(GROUPS) for a in range(PASSES)]
        units = [(g, c) for g in range(GROUPS) for c in range(CHUNKS)]
        offsets = keep.tile([P, S // LIST_ROWS], U16, name="offsets")
        tab = [kept([P, T], U32, "tab%d" % a) for a in range(PASSES)]
        tab_sc = kept([P, T], U8, "tab_sc")
        v = [kept([P, S], U32, "v%d" % a) for a in range(PASSES)]
        v_sc_rows = kept([P, S], U8, "v_sc_rows")
        v_sc = kept([P, S], U8, "v_sc")
        xs = kept([P, S], U32, "xs")
        xs_sc = kept([P, S], U8, "xs_sc")
        wg_raw = kept([P, FP4_BYTES * H], U8, "wg_raw")
        wg_sc_raw = kept([P, H], U8, "wg_sc_raw")
        wg = kept([P, FP4_BYTES * H], U8, "wg")
        wg_sc = kept([P, H], U8, "wg_sc")
        wc = kept([P, GROUPS * FP4_BYTES * N], U8, "wc")
        wc_sc = kept([P, GROUPS * N], U8, "wc_sc")
        bias = kept([P, GROUPS * PACK], F32, "bias")
        w1_raw = {piece: kept([P, PACK, KP], F32, "w1_raw%d%d" % piece) for piece in pieces}
        w1_bf = {piece: kept([P, PACK * KP], BF16, "w1_bf%d%d" % piece) for piece in pieces}
        w1q = {piece: kept([P, KP], U32, "w1q%d%d" % piece) for piece in pieces}
        w1_sc = {piece: kept([P, KP], U8, "w1_sc%d%d" % piece) for piece in pieces}
        wl_raw = [kept([P, PACK, N], F32, "wl_raw%d" % g) for g in range(GROUPS)]
        wl_bf = [kept([P, PACK * N], BF16, "wl_bf%d" % g) for g in range(GROUPS)]
        wlq = [kept([P, N], U32, "wlq%d" % g) for g in range(GROUPS)]
        wl_sc = [kept([P, N], U8, "wl_sc%d" % g) for g in range(GROUPS)]
        h = {unit: kept([P, PACK, CHUNK], F32, "h%d%d" % unit) for unit in units}
        hq = {unit: kept([P, CHUNK], U32, "hq%d%d" % unit) for unit in units}
        h_sc = {unit: kept([P, CHUNK], U8, "h_sc%d%d" % unit) for unit in units}
        zq = {unit: kept([P, CHUNK], U32, "zq%d%d" % unit) for unit in units}
        z_sc = {unit: kept([P, CHUNK], U8, "z_sc%d%d" % unit) for unit in units}
        damp = {(c, n): kept([P, CHUNK], F32, "damp%d%d" % (c, n)) for c in range(CHUNKS) for n in range(N_TILES)}

        def load_words(tile, words, lo, hi):
            nc.sync.dma_start(
                out=tile[:, lo:hi].bitcast(I32), in_=words[:, lo:hi, :].rearrange("p n t -> p (n t)").bitcast(I32)
            )

        def load_w1(a, g):
            nc.sync.dma_start(
                out=w1_raw[a, g][:],
                in_=w1[a * KP : (a + 1) * KP, g * KP : (g + 1) * KP].rearrange("(p j) c -> p j c", j=PACK),
            )

        def load_scales(queue, tile, scales):
            for r in range(QROWS):
                queue.dma_start(out=tile[r:P:QUAD, :].bitcast(I32), in_=scales[r::QROWS, :].bitcast(I32))

        def place_scales(rs):
            step = SPREAD * QROWS
            for r in rs:
                for a in range(PASSES):
                    first = SPREAD * (QROWS * QROWS * a + r)
                    nc.sync.dma_start(
                        out=v_sc[QROWS * a + r : P : QUAD, :].bitcast(I32),
                        in_=v_sc_rows[first : first + (QROWS - 1) * step + 1 : step, :].bitcast(I32),
                    )

        warm_in = kept([P, 1], F32, "warm_in")
        warm_out = kept([P, 1], F32, "warm_out")
        nc.gpsimd.memset(warm_in[:], 1.0)
        nc.scalar.activation(warm_out[:], warm_in[:], ACT.Abs_reciprocal_sqrt)

        for scale_tile in (tab_sc, wg_sc_raw, v_sc):
            nc.vector.memset(scale_tile[:].bitcast(I32), 0)
        for scale_tile in (xs_sc, wc_sc):
            nc.gpsimd.memset(scale_tile[:].bitcast(I32), 0)

        nc.gpsimd.dma_start(
            out=bias[:].rearrange("p (g t) -> p g t", t=PACK), in_=b1.rearrange("(g p t) -> p g t", g=GROUPS, t=PACK)
        )
        load_scales(nc.gpsimd, xs_sc, xs_scales[0])
        for r in range(QROWS):
            nc.gpsimd.dma_start(
                out=wc_sc[r:P:QUAD, :].bitcast(I32).rearrange("q (g n) -> q g n", g=GROUPS),
                in_=wc_scales[:, r::QROWS, :].bitcast(I32).rearrange("g q n -> q g n"),
            )

        nc.sync.dma_start(offsets[:], offs)
        nc.sync.dma_start(out=wg_raw[:].bitcast(I32), in_=wg_words[0].bitcast(I32))
        load_w1(0, 0)
        nc.sync.dma_start(
            out=tab_sc[0:P:SPREAD, :].bitcast(I32), in_=tab_scales.rearrange("a q n -> (a q) n").bitcast(I32)
        )
        load_scales(nc.sync, wg_sc_raw, wg_scales[0])
        load_words(tab[0], tab_words[0], 0, T)
        load_words(tab[1], tab_words[1], 0, T // 2)
        load_words(tab[1], tab_words[1], T // 2, T)
        nc.vector.tensor_copy(
            out=wg[:].rearrange("p (g t m b) -> p g t m b", g=GROUPS, t=PACK, b=FP4_BYTES),
            in_=wg_raw[:].rearrange("p (g m t b) -> p g t m b", g=GROUPS, t=PACK, b=FP4_BYTES),
        )
        nc.vector.tensor_copy(v_sc_rows[:], tab_sc[:].indirect(offsets[:]))
        place_scales(range(0, QROWS // 2))
        load_w1(1, 0)
        place_scales(range(QROWS // 2, QROWS))
        load_words(xs, xs_words[0], 0, S)
        load_w1(0, 1)
        load_w1(1, 1)
        for g in range(GROUPS):
            nc.sync.dma_start(
                out=wl_raw[g][:], in_=wl[g * KP : (g + 1) * KP, :].rearrange("(p j) n -> p j n", j=PACK)
            )
        nc.sync.dma_start(
            out=wc[:].bitcast(I32).rearrange("p (g n) -> p g n", g=GROUPS),
            in_=wc_words.bitcast(I32).rearrange("g p n -> p g n"),
        )

        nc.vector.tensor_copy(v[0][:], tab[0][:].indirect(offsets[:]))
        nc.vector.tensor_copy(
            out=wg_sc[:].rearrange("p (g t m) -> p g t m", g=GROUPS, t=PACK),
            in_=wg_sc_raw[:].rearrange("p (g m t) -> p g t m", g=GROUPS, t=PACK),
        )

        def quantise(codes, scales, values, lo, hi):
            nc.vector.quantize_mx(
                out=codes[:, lo:hi].bitcast(FP8X4), scales=scales[:, lo:hi], in_=values[:, PACK * lo : PACK * hi]
            )

        def quantise_w1(a, g, width):
            dst = w1_bf[a, g][:].rearrange("p (t m j) -> p m j t", t=PACK, j=PACK)
            src = w1_raw[a, g][:].rearrange("p j (m t) -> p m j t", t=PACK)
            share = W1_ON_VECTOR[a, g]
            if share > 0:
                nc.vector.tensor_copy(out=dst[:, :share], in_=src[:, :share])
            if share < P:
                nc.scalar.copy(out=dst[:, share:], in_=src[:, share:])
            for lo in range(0, KP, width):
                quantise(w1q[a, g], w1_sc[a, g], w1_bf[a, g], lo, lo + width)

        def first_stage(g, c, lo=0, hi=CHUNK, on_vector=()):
            cols = slice(c * CHUNK + lo, c * CHUNK + hi)
            for t in range(PACK):
                acc = acc_bank()
                for a in range(PASSES):
                    nc.tensor.matmul_mx(
                        out=acc[:, : hi - lo],
                        lhsT=w1q[a, g][:, t * P : (t + 1) * P].bitcast(FP8X4),
                        lhsT_scale=w1_sc[a, g][:, t * P : (t + 1) * P],
                        rhs=v[a][:, cols].bitcast(FP8X4),
                        rhs_scale=v_sc[QROWS * a : P, cols],
                        start=(a == 0),
                        stop=(a == PASSES - 1),
                    )
                b1_rows = bias[:, g * PACK + t : g * PACK + t + 1]
                if t in on_vector:
                    nc.vector.tensor_scalar(h[g, c][:, t, lo:hi], acc[:, : hi - lo], b1_rows, 0.0, ALU.add, ALU.max)
                else:
                    nc.scalar.activation(h[g, c][:, t, lo:hi], acc[:, : hi - lo], ACT.Relu, bias=b1_rows)

        def by_rows(ap):
            return ap.rearrange("p t (c i) -> p c t i", i=PAIR)

        def woven(ap):
            return ap.rearrange("p (c i t) -> p c t i", i=PAIR, t=PACK)

        def quantise_h(g, c, lo=0, hi=CHUNK):
            h_bf = ring.tile([P, PACK * CHUNK], BF16, name="h_bf", align_bytes=64)
            nc.vector.tensor_copy(out=woven(h_bf[:, PACK * lo : PACK * hi]), in_=by_rows(h[g, c][:, :, lo:hi]))
            quantise(hq[g, c], h_sc[g, c], h_bf, lo, hi)

        def stream_product(g, c):
            for j in range(0, CHUNK, BLK):
                cols = slice(c * CHUNK + j, c * CHUNK + j + BLK)
                b = psum.tile([P, PACK, BLK], F32, name="b%d" % (len(b_tiles) % B_BANKS))
                b_tiles[g, c, j] = b
                for t in range(PACK):
                    place = (g * PACK + t) * P
                    nc.tensor.matmul_mx(
                        out=b[:, t, :],
                        lhsT=wg[:, FP4_BYTES * place : FP4_BYTES * (place + P)].bitcast(FP4X4),
                        lhsT_scale=wg_sc[:, place : place + P],
                        rhs=xs[:, cols].bitcast(FP8X4),
                        rhs_scale=xs_sc[:, cols],
                        start=True,
                        stop=True,
                    )

        def quantise_z(g, c, lo=0, hi=CHUNK):
            z_bf = ring.tile([P, PACK * CHUNK], BF16, name="z_bf", align_bytes=64)
            for j in range(lo, hi, BLK):
                nc.vector.tensor_tensor(
                    woven(z_bf[:, PACK * j : PACK * (j + BLK)]),
                    by_rows(h[g, c][:, :, j : j + BLK]),
                    by_rows(b_tiles[g, c, j][:]),
                    ALU.subtract,
                )
            quantise(zq[g, c], z_sc[g, c], z_bf, lo, hi)

        def damping(c):
            for n in range(N_TILES):
                acc = acc_bank()
                for g in range(GROUPS):
                    col = g * N + n * P
                    nc.tensor.matmul_mx(
                        out=acc[:],
                        lhsT=wc[:, FP4_BYTES * col : FP4_BYTES * (col + P)].bitcast(FP4X4),
                        lhsT_scale=wc_sc[:, col : col + P],
                        rhs=hq[g, c][:].bitcast(FP8X4),
                        rhs_scale=h_sc[g, c][:],
                        start=(g == 0),
                        stop=(g == GROUPS - 1),
                    )
                root = ring.tile([P, CHUNK], F32, name="root")
                nc.scalar.activation(damp[c, n][:], acc[:], ACT.Abs)
                nc.scalar.activation(root[:], damp[c, n][:], ACT.Abs_reciprocal_sqrt, bias=1.0)
                nc.scalar.activation(damp[c, n][:], root[:], ACT.Square)

        def scores(c, lo=0, hi=CHUNK):
            for n in range(N_TILES):
                acc = acc_bank()
                for g in range(GROUPS):
                    nc.tensor.matmul_mx(
                        out=acc[:, : hi - lo],
                        lhsT=wlq[g][:, n * P : (n + 1) * P].bitcast(FP8X4),
                        lhsT_scale=wl_sc[g][:, n * P : (n + 1) * P],
                        rhs=zq[g, c][:, lo:hi].bitcast(FP8X4),
                        rhs_scale=z_sc[g, c][:, lo:hi],
                        start=(g == 0),
                        stop=(g == GROUPS - 1),
                    )
                res = ring.tile([P, CHUNK], F32, name="res", bufs=2 * N_TILES)
                nc.vector.tensor_tensor(res[:, : hi - lo], acc[:, : hi - lo], damp[c, n][:, lo:hi], ALU.mult)
                nc.sync.dma_start(
                    out=out[n * P : (n + 1) * P, c * CHUNK + lo : c * CHUNK + hi], in_=res[:, : hi - lo]
                )

        def quantise_wl(g):
            for n in range(0, N, P):
                nc.scalar.copy(
                    out=woven(wl_bf[g][:, PACK * n : PACK * (n + P)]), in_=by_rows(wl_raw[g][:, :, n : n + P])
                )
            quantise(wlq[g], wl_sc[g], wl_bf[g], 0, N)

        quantise_w1(0, 0, KP)
        nc.vector.tensor_copy(v[1][:], tab[1][:].indirect(offsets[:]))
        quantise_w1(1, 0, P)
        first_stage(0, 0, 0, HALF, on_vector=(2, 3))
        first_stage(0, 0, HALF, CHUNK)
        for g, c in units:
            stream_product(g, c)
        first_stage(0, 1)
        quantise_w1(0, 1, KP)
        quantise_w1(1, 1, KP)
        first_stage(1, 0)
        first_stage(1, 1)
        quantise_h(0, 0, 0, HALF)
        quantise_h(0, 0, HALF, CHUNK)
        quantise_h(0, 1)
        quantise_h(1, 0)
        quantise_h(1, 1)
        quantise_wl(0)
        quantise_wl(1)
        damping(0)
        damping(1)
        quantise_z(0, 0)
        quantise_z(0, 1)
        quantise_z(1, 0)
        scores(0)
        quantise_z(1, 1, 0, HALF)
        quantise_z(1, 1, HALF, CHUNK)
        scores(1, 0, HALF)
        scores(1, HALF, CHUNK)
